import numpy as np
import ml_dtypes


def mxq(x, axis, fmt="e4m3"):
    dtype, down = {"e4m3": (ml_dtypes.float8_e4m3fn, 7), "e5m2": (ml_dtypes.float8_e5m2, 14)}[fmt]
    v = np.moveaxis(np.asarray(x, np.float32).astype(ml_dtypes.bfloat16).astype(np.float64), axis, -1)
    blocks = v.reshape(v.shape[:-1] + (-1, 32))
    amax = np.abs(blocks).max(-1, keepdims=True)
    byte = np.maximum(np.where(amax > 0, np.frexp(amax)[1] - 1 + 127, 0) - down, 1)
    scale = np.exp2(byte - 127.0)
    codes = (blocks / scale).astype(np.float32).astype(dtype).astype(np.float64)
    return np.moveaxis((codes * scale).reshape(v.shape), -1, axis)


WIDE = False


def mx_kscale(k):
    if not WIDE:
        return np.ones(k)
    levels = np.array([10, -10, 5, -5, 0])
    if k % 512:
        return np.exp2(np.random.permutation(np.resize(levels, k // 32))).repeat(32)
    a = np.empty((k // 512, 16))
    for p in range(k // 512):
        a[p, :8] = np.random.permutation(np.resize(levels, 8))
        for g in range(8):
            far = levels[np.abs(levels - a[p, g]) >= 10]
            a[p, g + 8] = far[np.random.randint(len(far))]
    return np.exp2(a.ravel()).repeat(32)


def f64(x):
    return np.asarray(x).astype(np.float64)


def striped8(idx):
    return np.asarray(idx).reshape(8, -1, 16).transpose(0, 2, 1).reshape(128, -1).astype(np.uint16)


def unstriped8(offs):
    return offs.reshape(8, 16, -1).transpose(0, 2, 1).reshape(8, -1).astype(np.int64)


def pick8(x, idx, run):
    r = np.arange(len(x))
    return x[r[:, None], idx[r % (8 * run) // run]]


E2M1 = np.array([0.0, 0.5, 1.0, 1.5, 2.0, 3.0, 4.0, 6.0, -0.0, -0.5, -1.0, -1.5, -2.0, -3.0, -4.0, -6.0])


def pack_weight(w, fmt):
    k, n = w.shape
    w = f64(np.asarray(w, np.float32).astype(ml_dtypes.bfloat16)).reshape(k // 32, 32, n)
    amax = np.abs(w).max(1)
    if fmt == "e4m3":
        byte = np.frexp(amax)[1] - 1 + 127 - 7
    else:
        mant, ex = np.frexp(amax / 6.0)
        byte = np.where(mant > 0.5, ex, ex - 1) + 127
    byte = np.clip(np.where(amax > 0, byte, 1), 1, 254)
    scaled = (w * np.exp2(127.0 - byte)[:, None, :]).reshape(k, n).astype(np.float32)
    by_word = np.ascontiguousarray(scaled.reshape(k // 512, 128, 4, n).transpose(0, 1, 3, 2))
    if fmt == "e4m3":
        words = by_word.astype(ml_dtypes.float8_e4m3fn).view(np.uint8)
    else:
        c = by_word.astype(ml_dtypes.float4_e2m1fn).view(np.uint8) & 0xF
        words = (c[..., 0::2] | (c[..., 1::2] << 4)).reshape(k // 512, 128, 2 * n)
    return np.ascontiguousarray(words), np.ascontiguousarray(byte.astype(np.uint8).reshape(k // 512, 16, n))


def unpack_weight(words, scales, fmt):
    g, _, n = scales.shape
    words = np.ascontiguousarray(words).reshape(g, 128, n, -1)
    if fmt == "e4m3":
        vals = words.view(ml_dtypes.float8_e4m3fn).astype(np.float64)
    else:
        nib = np.empty((g, 128, n, 4), np.uint8)
        nib[..., 0::2] = words & 0xF
        nib[..., 1::2] = words >> 4
        vals = E2M1[nib]
    vals = vals * np.repeat(np.exp2(scales.astype(np.float64) - 127.0), 8, axis=1)[..., None]
    return vals.transpose(0, 1, 3, 2).reshape(g * 512, n)


def bf(x):
    return np.asarray(x, np.float32).astype(ml_dtypes.bfloat16)


def planes(Y):
    r, m = Y.shape
    b = f64(bf(Y)).reshape(r // 32, 32, m)
    amax = np.abs(b).max(1)
    byte = np.clip(np.where(amax > 0, np.frexp(amax)[1] - 1 + 127 - 7, 1), 1, 254)
    codes = (b * np.exp2(127.0 - byte)[:, None, :]).reshape(r, m).astype(np.float32).astype(ml_dtypes.float8_e4m3fn).view(np.uint8)
    words = codes.reshape(r // 512, 128, 4, m).transpose(0, 1, 3, 2)
    return np.ascontiguousarray(words), np.ascontiguousarray(byte.astype(np.uint8).reshape(r // 512, 16, m))


K, T, J, L, N = 512, 1024, 512, 512, 512


def setup_inputs():
    n = np.random.standard_normal
    idx = np.stack([np.random.permutation(T)[:J] for _ in range(8)])
    idx2 = np.stack([np.random.permutation(T)[:J] for _ in range(8)])
    fk = mx_kscale(K)
    fl = mx_kscale(L)
    wp = pack_weight(n((K, N)) * 1 / np.sqrt(K) * fk[:, None], "e4m3")
    bxp = pack_weight(n((L, J)) / fl[:, None], "e2m1")
    wbp = pack_weight(n((L, N)) * 1 / np.sqrt(L) * fl[:, None], "e4m3")
    return {
        "xf": (n((K, T)) / fk[:, None]).astype(np.float32),
        "w_words": wp[0],
        "w_scales": wp[1],
        "bx_words": bxp[0],
        "bx_scales": bxp[1],
        "wb_words": wbp[0],
        "wb_scales": wbp[1],
        "offs": striped8(idx),
        "offs2": striped8(idx2),
    }


def reference(xf, w_words, w_scales, bx_words, bx_scales, wb_words, wb_scales, offs, offs2):
    idx = unstriped8(offs)
    idx2 = unstriped8(offs2)
    wu = unpack_weight(w_words, w_scales, "e4m3")
    bxu = unpack_weight(bx_words, bx_scales, "e2m1")
    wbu = unpack_weight(wb_words, wb_scales, "e4m3")
    d = pick8(f64(xf), idx, 64) - pick8(f64(xf), idx2, 64)
    dq = mxq(d, 0, "e4m3")
    y = wu.T @ dq + wbu.T @ bxu
    words, scales = planes(y)
    return y, words, scales

@@ -1,0 +1,204 @@
+from contextlib import ExitStack
+
+import concourse.mybir as mybir
+
+K, T, J, L, N = 512, 1024, 512, 512, 512
+FLOPS = 2 * (K + L) * N * J
+
+F32 = mybir.dt.float32
+BF16 = mybir.dt.bfloat16
+I32 = mybir.dt.int32
+U32 = mybir.dt.uint32
+U16 = mybir.dt.uint16
+U8 = mybir.dt.uint8
+FP8X4 = mybir.dt.float8_e4m3fn_x4
+FP4X4 = mybir.dt.float4_e2m1fn_x4
+SUB = mybir.AluOpType.subtract
+
+P = 128
+PACK = 4
+HALF = J // 2
+QUARTER = J // 4
+LIST_COLS = HALF // 16
+W_ROW = 4
+
+
+def tile_list_head_changes_in_pl_kernel(
+    tc, xf, w_words, w_scales, bx_words, bx_scales, wb_words, wb_scales, offs, offs2, out_0, out_1, out_2
+):
+    nc = tc.nc
+    with ExitStack() as ctx:
+        keep = ctx.enter_context(tc.tile_pool(name="keep", bufs=1))
+        psum = ctx.enter_context(tc.psum_pool(name="psum", bufs=1))
+
+        list1 = keep.tile([P, J // 16], U16, name="list1")
+        list2 = keep.tile([P, J // 16], U16, name="list2")
+        planes = [keep.tile([P, T], F32, name=f"plane{t}") for t in range(PACK)]
+        raw_words = keep.tile([P, 2 * N], I32, name="raw_words", tag="raw_words", align_bytes=64)
+        raw_scales = keep.tile([P, N], U8, name="raw_scales", align_bytes=64)
+        bx_codes = keep.tile([P, 2 * J], U8, name="bx_codes", align_bytes=64)
+        bx_plane = keep.tile([P, J], U8, name="bx_plane", align_bytes=64)
+
+        nc.vector.memset(raw_scales[:].bitcast(U32), 0)
+        nc.vector.memset(bx_plane[:].bitcast(U32), 0)
+
+        xf_planes = xf.rearrange("(p t) c -> t p c", t=PACK)
+        nc.sync.dma_start(planes[0][:], xf_planes[0])
+        nc.sync.dma_start(list2[:], offs2)
+        nc.sync.dma_start(list1[:], offs)
+        for t in (1, 2):
+            nc.sync.dma_start(planes[t][:], xf_planes[t])
+        for q in range(4):
+            for row, scales in ((0, wb_scales), (W_ROW, w_scales)):
+                nc.sync.dma_start(
+                    raw_scales[32 * q + row : 32 * q + row + 4, :].bitcast(I32),
+                    scales[0, 4 * q : 4 * q + 4, :].bitcast(I32),
+                )
+        nc.sync.dma_start(planes[3][:], xf_planes[3])
+        for slot, words in ((1, wb_words), (0, w_words)):
+            nc.sync.dma_start(
+                raw_words[:, slot * N : (slot + 1) * N], words[0].rearrange("p n r -> p (n r)").bitcast(I32)
+            )
+        nc.sync.dma_start(bx_codes[:].bitcast(I32), bx_words[0].bitcast(I32))
+        for q in range(4):
+            nc.sync.dma_start(
+                bx_plane[32 * q : 32 * q + 4, :].bitcast(I32), bx_scales[0, 4 * q : 4 * q + 4, :].bitcast(I32)
+            )
+
+        picked = keep.tile([P, PACK * J], F32, name="picked", align_bytes=64)
+        d_woven = [keep.tile([P, PACK * HALF], BF16, name=f"d_woven{h}", align_bytes=64) for h in range(2)]
+        diff = {}
+
+        def pick(t, h):
+            cols = slice(h * LIST_COLS, (h + 1) * LIST_COLS)
+            at = t * J + h * HALF
+            nc.vector.tensor_copy(picked[:, at : at + HALF], planes[t][:].indirect(list2[:, cols]))
+
+        def subtract(t, h):
+            cols = slice(h * LIST_COLS, (h + 1) * LIST_COLS)
+            at = t * J + h * HALF
+            nc.vector.tensor_tensor(
+                diff[h, t // 2][:, (t % 2) * HALF : (t % 2 + 1) * HALF],
+                planes[t][:].indirect(list1[:, cols]),
+                picked[:, at : at + HALF],
+                SUB,
+            )
+
+        def pair_views(h, u, cols):
+            return (
+                d_woven[h][:].rearrange("p (c u e) -> p u c e", u=2, e=2)[:, u, cols, :],
+                diff[h, u][:].rearrange("p (e c) -> p c e", e=2)[:, cols, :],
+            )
+
+        diff[0, 0] = keep.tile([P, 2 * HALF], F32, name="diff00", align_bytes=64)
+        diff[0, 1] = keep.tile([P, 2 * HALF], F32, name="diff01", tag="late_pair", align_bytes=64)
+        for t in range(PACK):
+            pick(t, 0)
+            pick(t, 1)
+            subtract(t, 0)
+            if t % 2 == 1:
+                nc.scalar.copy(*pair_views(0, t // 2, slice(0, HALF)))
+
+        dealt_words = keep.tile([P, 2 * N], I32, name="dealt_words", align_bytes=64)
+        dealt_scales = keep.tile([P, N], U8, name="dealt_scales", align_bytes=64)
+        for slot in (1, 0):
+            nc.vector.tensor_copy(
+                dealt_words[:, slot * N : (slot + 1) * N].rearrange("p (t q) -> p q t", t=PACK),
+                raw_words[:, slot * N : (slot + 1) * N].rearrange("p (q t) -> p q t", t=PACK),
+            )
+        nc.vector.tensor_copy(
+            dealt_scales[:].rearrange("p (t q) -> p q t", t=PACK),
+            raw_scales[:].rearrange("p (q t) -> p q t", t=PACK),
+        )
+
+        banks = [psum.tile([P, PACK * QUARTER], F32, name=f"bank{b}") for b in range(4)]
+
+        def base_product(b):
+            for t in range(PACK):
+                nc.tensor.matmul_mx(
+                    out=banks[b][:, t * QUARTER : (t + 1) * QUARTER],
+                    lhsT=dealt_words[:, N + t * P : N + (t + 1) * P].bitcast(FP8X4),
+                    lhsT_scale=dealt_scales[:, t * P : (t + 1) * P],
+                    rhs=bx_codes[:, 2 * b * QUARTER : 2 * (b + 1) * QUARTER].bitcast(FP4X4),
+                    rhs_scale=bx_plane[:, b * QUARTER : (b + 1) * QUARTER],
+                    start=(t == 0),
+                    stop=False,
+                )
+
+        base_product(0)
+        base_product(1)
+        d_codes = keep.tile([P, J], U32, name="d_codes", align_bytes=64)
+        d_scales = keep.tile([P, J], U8, name="d_scales", align_bytes=64)
+        y_first = keep.tile([P, PACK, HALF], F32, name="y_first", align_bytes=64)
+        y_last = [keep.tile([P, PACK * QUARTER], F32, name=f"y_last{i}", align_bytes=64) for i in range(2)]
+        y_woven = [keep.tile([P, PACK * HALF], BF16, name=f"y_woven{h}", align_bytes=64) for h in range(2)]
+        y_codes = keep.tile([P, J], U32, name="y_codes", align_bytes=64)
+        y_scales = keep.tile([P, J], U8, name="y_scales", align_bytes=64)
+        out_rows = out_0.rearrange("(p t) j -> p t j", t=PACK)
+        out_words = out_1[0].rearrange("p j r -> p (j r)").bitcast(I32)
+
+        def quantize_d(src, cols):
+            nc.vector.quantize_mx(out=d_codes[:, cols].bitcast(FP8X4), scales=d_scales[:, cols], in_=src)
+
+        def multiply(b):
+            cols = slice(b * QUARTER, (b + 1) * QUARTER)
+            for t in range(PACK):
+                nc.tensor.matmul_mx(
+                    out=banks[b][:, t * QUARTER : (t + 1) * QUARTER],
+                    lhsT=dealt_words[:, t * P : (t + 1) * P].bitcast(FP8X4),
+                    lhsT_scale=dealt_scales[W_ROW:P, t * P : (t + 1) * P],
+                    rhs=d_codes[:, cols].bitcast(FP8X4),
+                    rhs_scale=d_scales[:, cols],
+                    start=False,
+                    stop=(t == PACK - 1),
+                )
+
+        def y_views(b):
+            at = (b % 2) * PACK * QUARTER
+            return (
+                y_woven[b // 2][:, at : at + PACK * QUARTER].rearrange("p (c t) -> p c t", t=PACK),
+                banks[b][:].rearrange("p (t c) -> p c t", t=PACK),
+            )
+
+        def quantize_y(h):
+            cols = slice(h * HALF, (h + 1) * HALF)
+            nc.vector.quantize_mx(out=y_codes[:, cols].bitcast(FP8X4), scales=y_scales[:, cols], in_=y_woven[h][:])
+            nc.sync.dma_start(out_words[:, cols], y_codes[:, cols].bitcast(I32))
+
+        diff[1, 0] = keep.tile([P, 2 * HALF], F32, name="diff10", tag="raw_words", align_bytes=64)
+        diff[1, 1] = keep.tile([P, 2 * HALF], F32, name="diff11", tag="late_pair", align_bytes=64)
+        quantize_d(d_woven[0][:], slice(0, HALF))
+        subtract(0, 1)
+        subtract(1, 1)
+        nc.scalar.copy(*pair_views(1, 0, slice(0, HALF)))
+        for b in range(2):
+            multiply(b)
+            nc.scalar.copy(
+                y_first[:, :, b * QUARTER : (b + 1) * QUARTER], banks[b][:].rearrange("p (t c) -> p t c", t=PACK)
+            )
+            dst, src = y_views(b)
+            nc.scalar.copy(dst, src)
+        nc.sync.dma_start(out_rows[:, :, 0:HALF], y_first[:])
+        base_product(2)
+        base_product(3)
+        subtract(2, 1)
+        subtract(3, 1)
+
+        for i in range(2):
+            nc.vector.tensor_copy(*pair_views(1, 1, slice(i * QUARTER, (i + 1) * QUARTER)))
+        for i in range(2):
+            quantize_d(d_woven[1][:, i * PACK * QUARTER : (i + 1) * PACK * QUARTER], slice(HALF + i * QUARTER, HALF + (i + 1) * QUARTER))
+            multiply(2 + i)
+        quantize_y(0)
+        for i in range(2):
+            dst, src = y_views(2 + i)
+            nc.vector.tensor_copy(dst, src)
+            nc.scalar.copy(y_last[i][:], banks[2 + i][:])
+            nc.sync.dma_start(
+                out_rows[:, :, HALF + i * QUARTER : HALF + (i + 1) * QUARTER],
+                y_last[i][:].rearrange("p (t c) -> p t c", t=PACK),
+            )
+        quantize_y(1)
+        for q in range(4):
+            queue = nc.sync if q % 2 == 0 else nc.scalar
+            queue.dma_start(out_2[0, 4 * q : 4 * q + 4, :].bitcast(I32), y_scales[32 * q : 32 * q + 4, :].bitcast(I32))

@@ -34,7 +34,7 @@ def tile_list_head_changes_in_pl_kernel(
         list1 = keep.tile([P, J // 16], U16, name="list1")
         list2 = keep.tile([P, J // 16], U16, name="list2")
         planes = [keep.tile([P, T], F32, name=f"plane{t}") for t in range(PACK)]
-        raw_words = keep.tile([P, 2 * N], I32, name="raw_words", tag="raw_words", align_bytes=64)
+        raw_words = keep.tile([P, 2 * N], I32, name="raw_words", align_bytes=64)
         raw_scales = keep.tile([P, N], U8, name="raw_scales", align_bytes=64)
         bx_codes = keep.tile([P, 2 * J], U8, name="bx_codes", align_bytes=64)
         bx_plane = keep.tile([P, J], U8, name="bx_plane", align_bytes=64)
@@ -46,7 +46,12 @@ def tile_list_head_changes_in_pl_kernel(
         nc.sync.dma_start(planes[0][:], xf_planes[0])
         nc.sync.dma_start(list2[:], offs2)
         nc.sync.dma_start(list1[:], offs)
-        for t in (1, 2):
+        nc.sync.dma_start(planes[1][:], xf_planes[1])
+        for slot, words in ((1, wb_words), (0, w_words)):
+            nc.sync.dma_start(
+                raw_words[:, slot * N : (slot + 1) * N], words[0].rearrange("p n r -> p (n r)").bitcast(I32)
+            )
+        for t in range(2, PACK):
             nc.sync.dma_start(planes[t][:], xf_planes[t])
         for q in range(4):
             for row, scales in ((0, wb_scales), (W_ROW, w_scales)):
@@ -54,61 +59,65 @@ def tile_list_head_changes_in_pl_kernel(
                     raw_scales[32 * q + row : 32 * q + row + 4, :].bitcast(I32),
                     scales[0, 4 * q : 4 * q + 4, :].bitcast(I32),
                 )
-        nc.sync.dma_start(planes[3][:], xf_planes[3])
-        for slot, words in ((1, wb_words), (0, w_words)):
-            nc.sync.dma_start(
-                raw_words[:, slot * N : (slot + 1) * N], words[0].rearrange("p n r -> p (n r)").bitcast(I32)
-            )
         nc.sync.dma_start(bx_codes[:].bitcast(I32), bx_words[0].bitcast(I32))
         for q in range(4):
             nc.sync.dma_start(
                 bx_plane[32 * q : 32 * q + 4, :].bitcast(I32), bx_scales[0, 4 * q : 4 * q + 4, :].bitcast(I32)
             )
 
-        picked = keep.tile([P, PACK * J], F32, name="picked", align_bytes=64)
+        picked = keep.tile([P, (2 * PACK + 1) * HALF], F32, name="picked", align_bytes=64)
         d_woven = [keep.tile([P, PACK * HALF], BF16, name=f"d_woven{h}", align_bytes=64) for h in range(2)]
         diff = {}
 
+        def picked_slot(t, h):
+            at = (2 * t + 1 - h) * HALF
+            return picked[:, at : at + HALF]
+
         def pick(t, h):
             cols = slice(h * LIST_COLS, (h + 1) * LIST_COLS)
-            at = t * J + h * HALF
-            nc.vector.tensor_copy(picked[:, at : at + HALF], planes[t][:].indirect(list2[:, cols]))
+            nc.vector.tensor_copy(picked_slot(t, h), planes[t][:].indirect(list2[:, cols]))
 
         def subtract(t, h):
             cols = slice(h * LIST_COLS, (h + 1) * LIST_COLS)
-            at = t * J + h * HALF
             nc.vector.tensor_tensor(
                 diff[h, t // 2][:, (t % 2) * HALF : (t % 2 + 1) * HALF],
                 planes[t][:].indirect(list1[:, cols]),
-                picked[:, at : at + HALF],
+                picked_slot(t, h),
                 SUB,
             )
 
         def pair_views(h, u, cols):
             return (
                 d_woven[h][:].rearrange("p (c u e) -> p u c e", u=2, e=2)[:, u, cols, :],
-                diff[h, u][:].rearrange("p (e c) -> p c e", e=2)[:, cols, :],
+                diff[h, u].rearrange("p (e c) -> p c e", e=2)[:, cols, :],
             )
 
-        diff[0, 0] = keep.tile([P, 2 * HALF], F32, name="diff00", align_bytes=64)
-        diff[0, 1] = keep.tile([P, 2 * HALF], F32, name="diff01", tag="late_pair", align_bytes=64)
+        early_pair = keep.tile([P, 2 * HALF], F32, name="early_pair", align_bytes=64)
+        late_pair = keep.tile([P, 2 * HALF], F32, name="late_pair", align_bytes=64)
+        diff[0, 0] = early_pair[:]
+        diff[0, 1] = late_pair[:]
+        diff[1, 1] = picked[:, (2 * PACK - 1) * HALF : (2 * PACK + 1) * HALF]
+        diff[1, 0] = late_pair[:]
         for t in range(PACK):
             pick(t, 0)
             pick(t, 1)
             subtract(t, 0)
             if t % 2 == 1:
                 nc.scalar.copy(*pair_views(0, t // 2, slice(0, HALF)))
+        subtract(3, 1)
+        subtract(2, 1)
+        nc.scalar.copy(*pair_views(1, 1, slice(0, HALF)))
 
         dealt_words = keep.tile([P, 2 * N], I32, name="dealt_words", align_bytes=64)
         dealt_scales = keep.tile([P, N], U8, name="dealt_scales", align_bytes=64)
         for slot in (1, 0):
-            nc.vector.tensor_copy(
-                dealt_words[:, slot * N : (slot + 1) * N].rearrange("p (t q) -> p q t", t=PACK),
-                raw_words[:, slot * N : (slot + 1) * N].rearrange("p (q t) -> p q t", t=PACK),
+            nc.gpsimd.tensor_copy(
+                dealt_words[:, slot * N : (slot + 1) * N].rearrange("p (t q) -> p t q", t=PACK),
+                raw_words[:, slot * N : (slot + 1) * N].rearrange("p (q t) -> p t q", t=PACK),
             )
-        nc.vector.tensor_copy(
-            dealt_scales[:].rearrange("p (t q) -> p q t", t=PACK),
-            raw_scales[:].rearrange("p (q t) -> p q t", t=PACK),
+        nc.gpsimd.tensor_copy(
+            dealt_scales[:].rearrange("p (t q) -> p t q", t=PACK),
+            raw_scales[:].rearrange("p (q t) -> p t q", t=PACK),
         )
 
         banks = [psum.tile([P, PACK * QUARTER], F32, name=f"bank{b}") for b in range(4)]
@@ -165,31 +174,25 @@ def tile_list_head_changes_in_pl_kernel(
             nc.vector.quantize_mx(out=y_codes[:, cols].bitcast(FP8X4), scales=y_scales[:, cols], in_=y_woven[h][:])
             nc.sync.dma_start(out_words[:, cols], y_codes[:, cols].bitcast(I32))
 
-        diff[1, 0] = keep.tile([P, 2 * HALF], F32, name="diff10", tag="raw_words", align_bytes=64)
-        diff[1, 1] = keep.tile([P, 2 * HALF], F32, name="diff11", tag="late_pair", align_bytes=64)
         quantize_d(d_woven[0][:], slice(0, HALF))
         subtract(0, 1)
         subtract(1, 1)
-        nc.scalar.copy(*pair_views(1, 0, slice(0, HALF)))
         for b in range(2):
             multiply(b)
             nc.scalar.copy(
                 y_first[:, :, b * QUARTER : (b + 1) * QUARTER], banks[b][:].rearrange("p (t c) -> p t c", t=PACK)
             )
-            dst, src = y_views(b)
-            nc.scalar.copy(dst, src)
         nc.sync.dma_start(out_rows[:, :, 0:HALF], y_first[:])
+        for b in range(2):
+            nc.scalar.copy(*y_views(b))
         base_product(2)
         base_product(3)
-        subtract(2, 1)
-        subtract(3, 1)
 
         for i in range(2):
-            nc.vector.tensor_copy(*pair_views(1, 1, slice(i * QUARTER, (i + 1) * QUARTER)))
+            nc.vector.tensor_copy(*pair_views(1, 0, slice(i * QUARTER, (i + 1) * QUARTER)))
         for i in range(2):
             quantize_d(d_woven[1][:, i * PACK * QUARTER : (i + 1) * PACK * QUARTER], slice(HALF + i * QUARTER, HALF + (i + 1) * QUARTER))
             multiply(2 + i)
-        quantize_y(0)
         for i in range(2):
             dst, src = y_views(2 + i)
             nc.vector.tensor_copy(dst, src)
@@ -198,6 +201,7 @@ def tile_list_head_changes_in_pl_kernel(
                 out_rows[:, :, HALF + i * QUARTER : HALF + (i + 1) * QUARTER],
                 y_last[i][:].rearrange("p (t c) -> p t c", t=PACK),
             )
+        quantize_y(0)
         quantize_y(1)
         for q in range(4):
             queue = nc.sync if q % 2 == 0 else nc.scalar

@@ -17,10 +17,14 @@ SUB = mybir.AluOpType.subtract
 
 P = 128
 PACK = 4
+QUADRANTS = 4
 HALF = J // 2
 QUARTER = J // 4
 LIST_COLS = HALF // 16
 W_ROW = 4
+LINE = 4
+ALIGN = 64
+W_SIDE, WB_SIDE = 0, 1
 
 
 def tile_list_head_changes_in_pl_kernel(
@@ -34,55 +38,61 @@ def tile_list_head_changes_in_pl_kernel(
         list1 = keep.tile([P, J // 16], U16, name="list1")
         list2 = keep.tile([P, J // 16], U16, name="list2")
         planes = [keep.tile([P, T], F32, name=f"plane{t}") for t in range(PACK)]
-        raw_words = keep.tile([P, 2 * N], I32, name="raw_words", align_bytes=64)
-        raw_scales = keep.tile([P, N], U8, name="raw_scales", align_bytes=64)
-        bx_codes = keep.tile([P, 2 * J], U8, name="bx_codes", align_bytes=64)
-        bx_plane = keep.tile([P, J], U8, name="bx_plane", align_bytes=64)
+        raw_words = keep.tile([P, 2 * N], I32, name="raw_words", align_bytes=ALIGN)
+        raw_scales = keep.tile([P, N], U8, name="raw_scales", align_bytes=ALIGN)
+        bx_codes = keep.tile([P, 2 * J], U8, name="bx_codes", align_bytes=ALIGN)
+        bx_plane = keep.tile([P, J], U8, name="bx_plane", align_bytes=ALIGN)
 
         nc.vector.memset(raw_scales[:].bitcast(U32), 0)
         nc.vector.memset(bx_plane[:].bitcast(U32), 0)
+
+        def load_scale_rows(tile, first_row, scales, q):
+            at = 32 * q + first_row
+            nc.sync.dma_start(tile[at : at + 4, :].bitcast(I32), scales[0, 4 * q : 4 * q + 4, :].bitcast(I32))
 
         xf_planes = xf.rearrange("(p t) c -> t p c", t=PACK)
         nc.sync.dma_start(planes[0][:], xf_planes[0])
         nc.sync.dma_start(list2[:], offs2)
         nc.sync.dma_start(list1[:], offs)
         nc.sync.dma_start(planes[1][:], xf_planes[1])
-        for slot, words in ((1, wb_words), (0, w_words)):
+        for side, words in ((WB_SIDE, wb_words), (W_SIDE, w_words)):
             nc.sync.dma_start(
-                raw_words[:, slot * N : (slot + 1) * N], words[0].rearrange("p n r -> p (n r)").bitcast(I32)
+                raw_words[:, side * N : (side + 1) * N], words[0].rearrange("p n r -> p (n r)").bitcast(I32)
             )
         for t in range(2, PACK):
             nc.sync.dma_start(planes[t][:], xf_planes[t])
-        for q in range(4):
-            for row, scales in ((0, wb_scales), (W_ROW, w_scales)):
-                nc.sync.dma_start(
-                    raw_scales[32 * q + row : 32 * q + row + 4, :].bitcast(I32),
-                    scales[0, 4 * q : 4 * q + 4, :].bitcast(I32),
-                )
+        for q in range(QUADRANTS):
+            load_scale_rows(raw_scales, 0, wb_scales, q)
+            load_scale_rows(raw_scales, W_ROW, w_scales, q)
         nc.sync.dma_start(bx_codes[:].bitcast(I32), bx_words[0].bitcast(I32))
-        for q in range(4):
-            nc.sync.dma_start(
-                bx_plane[32 * q : 32 * q + 4, :].bitcast(I32), bx_scales[0, 4 * q : 4 * q + 4, :].bitcast(I32)
-            )
+        for q in range(QUADRANTS):
+            load_scale_rows(bx_plane, 0, bx_scales, q)
 
-        picked = keep.tile([P, (2 * PACK + 1) * HALF], F32, name="picked", align_bytes=64)
-        d_woven = [keep.tile([P, PACK * HALF], BF16, name=f"d_woven{h}", align_bytes=64) for h in range(2)]
-        diff = {}
+        picked = keep.tile([P, (2 * PACK + 1) * HALF], F32, name="picked", align_bytes=ALIGN)
+        d_woven = [keep.tile([P, PACK * HALF], BF16, name=f"d_woven{h}", align_bytes=ALIGN) for h in range(2)]
+        early_pair = keep.tile([P, 2 * HALF], F32, name="early_pair", align_bytes=ALIGN)
+        late_pair = keep.tile([P, 2 * HALF], F32, name="late_pair", align_bytes=ALIGN)
+        diff = {
+            (0, 0): early_pair[:],
+            (0, 1): late_pair[:],
+            (1, 1): picked[:, (2 * PACK - 1) * HALF : (2 * PACK + 1) * HALF],
+            (1, 0): late_pair[:],
+        }
 
-        def picked_slot(t, h):
+        def picked_place(t, h):
             at = (2 * t + 1 - h) * HALF
             return picked[:, at : at + HALF]
 
         def pick(t, h):
             cols = slice(h * LIST_COLS, (h + 1) * LIST_COLS)
-            nc.vector.tensor_copy(picked_slot(t, h), planes[t][:].indirect(list2[:, cols]))
+            nc.vector.tensor_copy(picked_place(t, h), planes[t][:].indirect(list2[:, cols]))
 
         def subtract(t, h):
             cols = slice(h * LIST_COLS, (h + 1) * LIST_COLS)
             nc.vector.tensor_tensor(
                 diff[h, t // 2][:, (t % 2) * HALF : (t % 2 + 1) * HALF],
                 planes[t][:].indirect(list1[:, cols]),
-                picked_slot(t, h),
+                picked_place(t, h),
                 SUB,
             )
 
@@ -92,12 +102,6 @@ def tile_list_head_changes_in_pl_kernel(
                 diff[h, u].rearrange("p (e c) -> p c e", e=2)[:, cols, :],
             )
 
-        early_pair = keep.tile([P, 2 * HALF], F32, name="early_pair", align_bytes=64)
-        late_pair = keep.tile([P, 2 * HALF], F32, name="late_pair", align_bytes=64)
-        diff[0, 0] = early_pair[:]
-        diff[0, 1] = late_pair[:]
-        diff[1, 1] = picked[:, (2 * PACK - 1) * HALF : (2 * PACK + 1) * HALF]
-        diff[1, 0] = late_pair[:]
         for t in range(PACK):
             pick(t, 0)
             pick(t, 1)
@@ -108,25 +112,26 @@ def tile_list_head_changes_in_pl_kernel(
         subtract(2, 1)
         nc.scalar.copy(*pair_views(1, 1, slice(0, HALF)))
 
-        dealt_words = keep.tile([P, 2 * N], I32, name="dealt_words", align_bytes=64)
-        dealt_scales = keep.tile([P, N], U8, name="dealt_scales", align_bytes=64)
-        for slot in (1, 0):
+        dealt_words = keep.tile([P, 2 * N], I32, name="dealt_words", align_bytes=ALIGN)
+        dealt_scales = keep.tile([P, N], U8, name="dealt_scales", align_bytes=ALIGN)
+        for side in (WB_SIDE, W_SIDE):
             nc.gpsimd.tensor_copy(
-                dealt_words[:, slot * N : (slot + 1) * N].rearrange("p (t q) -> p t q", t=PACK),
-                raw_words[:, slot * N : (slot + 1) * N].rearrange("p (q t) -> p t q", t=PACK),
+                dealt_words[:, side * N : (side + 1) * N].rearrange("p (t q) -> p t q", t=PACK),
+                raw_words[:, side * N : (side + 1) * N].rearrange("p (q t) -> p t q", t=PACK),
             )
         nc.gpsimd.tensor_copy(
             dealt_scales[:].rearrange("p (t q) -> p t q", t=PACK),
             raw_scales[:].rearrange("p (q t) -> p t q", t=PACK),
         )
 
-        banks = [psum.tile([P, PACK * QUARTER], F32, name=f"bank{b}") for b in range(4)]
+        banks = [psum.tile([P, PACK * QUARTER], F32, name=f"bank{b}") for b in range(J // QUARTER)]
 
         def base_product(b):
             for t in range(PACK):
+                at = WB_SIDE * N + t * P
                 nc.tensor.matmul_mx(
                     out=banks[b][:, t * QUARTER : (t + 1) * QUARTER],
-                    lhsT=dealt_words[:, N + t * P : N + (t + 1) * P].bitcast(FP8X4),
+                    lhsT=dealt_words[:, at : at + P].bitcast(FP8X4),
                     lhsT_scale=dealt_scales[:, t * P : (t + 1) * P],
                     rhs=bx_codes[:, 2 * b * QUARTER : 2 * (b + 1) * QUARTER].bitcast(FP4X4),
                     rhs_scale=bx_plane[:, b * QUARTER : (b + 1) * QUARTER],
@@ -136,25 +141,26 @@ def tile_list_head_changes_in_pl_kernel(
 
         base_product(0)
         base_product(1)
-        d_codes = keep.tile([P, J], U32, name="d_codes", align_bytes=64)
-        d_scales = keep.tile([P, J], U8, name="d_scales", align_bytes=64)
-        y_first = keep.tile([P, PACK, HALF], F32, name="y_first", align_bytes=64)
-        y_last = [keep.tile([P, PACK * QUARTER], F32, name=f"y_last{i}", align_bytes=64) for i in range(2)]
-        y_woven = [keep.tile([P, PACK * HALF], BF16, name=f"y_woven{h}", align_bytes=64) for h in range(2)]
-        y_codes = keep.tile([P, J], U32, name="y_codes", align_bytes=64)
-        y_scales = keep.tile([P, J], U8, name="y_scales", align_bytes=64)
+        d_codes = keep.tile([P, J], U32, name="d_codes", align_bytes=ALIGN)
+        d_scales = keep.tile([P, J], U8, name="d_scales", align_bytes=ALIGN)
+        y_first = keep.tile([P, PACK, HALF], F32, name="y_first", align_bytes=ALIGN)
+        y_last = [keep.tile([P, PACK * QUARTER], F32, name=f"y_last{i}", align_bytes=ALIGN) for i in range(2)]
+        y_woven = [keep.tile([P, PACK * HALF], BF16, name=f"y_woven{h}", align_bytes=ALIGN) for h in range(2)]
+        y_codes = keep.tile([P, J], U32, name="y_codes", align_bytes=ALIGN)
+        y_scales = keep.tile([P, J], U8, name="y_scales", align_bytes=ALIGN)
         out_rows = out_0.rearrange("(p t) j -> p t j", t=PACK)
         out_words = out_1[0].rearrange("p j r -> p (j r)").bitcast(I32)
 
         def quantize_d(src, cols):
             nc.vector.quantize_mx(out=d_codes[:, cols].bitcast(FP8X4), scales=d_scales[:, cols], in_=src)
 
-        def multiply(b):
+        def change_product(b):
             cols = slice(b * QUARTER, (b + 1) * QUARTER)
             for t in range(PACK):
+                at = W_SIDE * N + t * P
                 nc.tensor.matmul_mx(
                     out=banks[b][:, t * QUARTER : (t + 1) * QUARTER],
-                    lhsT=dealt_words[:, t * P : (t + 1) * P].bitcast(FP8X4),
+                    lhsT=dealt_words[:, at : at + P].bitcast(FP8X4),
                     lhsT_scale=dealt_scales[W_ROW:P, t * P : (t + 1) * P],
                     rhs=d_codes[:, cols].bitcast(FP8X4),
                     rhs_scale=d_scales[:, cols],
@@ -162,47 +168,57 @@ def tile_list_head_changes_in_pl_kernel(
                     stop=(t == PACK - 1),
                 )
 
-        def y_views(b):
-            at = (b % 2) * PACK * QUARTER
-            return (
-                y_woven[b // 2][:, at : at + PACK * QUARTER].rearrange("p (c t) -> p c t", t=PACK),
-                banks[b][:].rearrange("p (t c) -> p c t", t=PACK),
+        def woven_quarters(first, count):
+            at = (first % 2) * PACK * QUARTER
+            return y_woven[first // 2][:, at : at + count * PACK * QUARTER]
+
+        def weave_y(b, rows):
+            nc.vector.tensor_copy(
+                woven_quarters(b, 1).rearrange("p (c i t) -> p c t i", t=PACK, i=LINE),
+                rows.rearrange("p t (c i) -> p c t i", i=LINE),
             )
 
-        def quantize_y(h):
-            cols = slice(h * HALF, (h + 1) * HALF)
-            nc.vector.quantize_mx(out=y_codes[:, cols].bitcast(FP8X4), scales=y_scales[:, cols], in_=y_woven[h][:])
-            nc.sync.dma_start(out_words[:, cols], y_codes[:, cols].bitcast(I32))
+        def quantize_y(first, count):
+            cols = slice(first * QUARTER, (first + count) * QUARTER)
+            nc.vector.quantize_mx(
+                out=y_codes[:, cols].bitcast(FP8X4), scales=y_scales[:, cols], in_=woven_quarters(first, count)
+            )
 
         quantize_d(d_woven[0][:], slice(0, HALF))
         subtract(0, 1)
         subtract(1, 1)
         for b in range(2):
-            multiply(b)
+            change_product(b)
             nc.scalar.copy(
                 y_first[:, :, b * QUARTER : (b + 1) * QUARTER], banks[b][:].rearrange("p (t c) -> p t c", t=PACK)
             )
         nc.sync.dma_start(out_rows[:, :, 0:HALF], y_first[:])
-        for b in range(2):
-            nc.scalar.copy(*y_views(b))
+        nc.scalar.copy(
+            woven_quarters(0, 1).rearrange("p (c t) -> p c t", t=PACK),
+            banks[0][:].rearrange("p (t c) -> p c t", t=PACK),
+        )
         base_product(2)
         base_product(3)
 
         for i in range(2):
             nc.vector.tensor_copy(*pair_views(1, 0, slice(i * QUARTER, (i + 1) * QUARTER)))
         for i in range(2):
-            quantize_d(d_woven[1][:, i * PACK * QUARTER : (i + 1) * PACK * QUARTER], slice(HALF + i * QUARTER, HALF + (i + 1) * QUARTER))
-            multiply(2 + i)
-        for i in range(2):
-            dst, src = y_views(2 + i)
-            nc.vector.tensor_copy(dst, src)
-            nc.scalar.copy(y_last[i][:], banks[2 + i][:])
-            nc.sync.dma_start(
-                out_rows[:, :, HALF + i * QUARTER : HALF + (i + 1) * QUARTER],
-                y_last[i][:].rearrange("p (t c) -> p t c", t=PACK),
+            quantize_d(
+                d_woven[1][:, i * PACK * QUARTER : (i + 1) * PACK * QUARTER],
+                slice(HALF + i * QUARTER, HALF + (i + 1) * QUARTER),
             )
-        quantize_y(0)
-        quantize_y(1)
-        for q in range(4):
+            change_product(2 + i)
+        weave_y(1, y_first[:, :, QUARTER:HALF])
+        quantize_y(0, 2)
+        nc.sync.dma_start(out_words[:, 0:HALF], y_codes[:, 0:HALF].bitcast(I32))
+        for i in range(2):
+            nc.scalar.copy(y_last[i][:], banks[2 + i][:])
+            rows = y_last[i][:].rearrange("p (t c) -> p t c", t=PACK)
+            nc.sync.dma_start(out_rows[:, :, HALF + i * QUARTER : HALF + (i + 1) * QUARTER], rows)
+            weave_y(2 + i, rows)
+        for i in range(2):
+            quantize_y(2 + i, 1)
+        nc.sync.dma_start(out_words[:, HALF:J], y_codes[:, HALF:J].bitcast(I32))
+        for q in range(QUADRANTS):
             queue = nc.sync if q % 2 == 0 else nc.scalar
             queue.dma_start(out_2[0, 4 * q : 4 * q + 4, :].bitcast(I32), y_scales[32 * q : 32 * q + 4, :].bitcast(I32))

from contextlib import ExitStack

import concourse.mybir as mybir

K, T, J, L, N = 512, 1024, 512, 512, 512
FLOPS = 2 * (K + L) * N * J

F32 = mybir.dt.float32
BF16 = mybir.dt.bfloat16
I32 = mybir.dt.int32
U32 = mybir.dt.uint32
U16 = mybir.dt.uint16
U8 = mybir.dt.uint8
FP8X4 = mybir.dt.float8_e4m3fn_x4
FP4X4 = mybir.dt.float4_e2m1fn_x4
SUB = mybir.AluOpType.subtract

P = 128
PACK = 4
QUADRANTS = 4
HALF = J // 2
QUARTER = J // 4
LIST_COLS = HALF // 16
W_ROW = 4
LINE = 4
ALIGN = 64
W_SIDE, WB_SIDE = 0, 1


def tile_list_head_changes_in_pl_kernel(
    tc, xf, w_words, w_scales, bx_words, bx_scales, wb_words, wb_scales, offs, offs2, out_0, out_1, out_2
):
    nc = tc.nc
    with ExitStack() as ctx:
        keep = ctx.enter_context(tc.tile_pool(name="keep", bufs=1))
        psum = ctx.enter_context(tc.psum_pool(name="psum", bufs=1))

        list1 = keep.tile([P, J // 16], U16, name="list1")
        list2 = keep.tile([P, J // 16], U16, name="list2")
        planes = [keep.tile([P, T], F32, name=f"plane{t}") for t in range(PACK)]
        raw_words = keep.tile([P, 2 * N], I32, name="raw_words", align_bytes=ALIGN)
        raw_scales = keep.tile([P, N], U8, name="raw_scales", align_bytes=ALIGN)
        bx_codes = keep.tile([P, 2 * J], U8, name="bx_codes", align_bytes=ALIGN)
        bx_plane = keep.tile([P, J], U8, name="bx_plane", align_bytes=ALIGN)

        nc.vector.memset(raw_scales[:].bitcast(U32), 0)
        nc.vector.memset(bx_plane[:].bitcast(U32), 0)

        def load_scale_rows(tile, first_row, scales, q):
            at = 32 * q + first_row
            nc.sync.dma_start(tile[at : at + 4, :].bitcast(I32), scales[0, 4 * q : 4 * q + 4, :].bitcast(I32))

        xf_planes = xf.rearrange("(p t) c -> t p c", t=PACK)
        nc.sync.dma_start(planes[0][:], xf_planes[0])
        nc.sync.dma_start(list2[:], offs2)
        nc.sync.dma_start(list1[:], offs)
        nc.sync.dma_start(planes[1][:], xf_planes[1])
        for side, words in ((WB_SIDE, wb_words), (W_SIDE, w_words)):
            nc.sync.dma_start(
                raw_words[:, side * N : (side + 1) * N], words[0].rearrange("p n r -> p (n r)").bitcast(I32)
            )
        for t in range(2, PACK):
            nc.sync.dma_start(planes[t][:], xf_planes[t])
        for q in range(QUADRANTS):
            load_scale_rows(raw_scales, 0, wb_scales, q)
            load_scale_rows(raw_scales, W_ROW, w_scales, q)
        nc.sync.dma_start(bx_codes[:].bitcast(I32), bx_words[0].bitcast(I32))
        for q in range(QUADRANTS):
            load_scale_rows(bx_plane, 0, bx_scales, q)

        picked = keep.tile([P, (2 * PACK + 1) * HALF], F32, name="picked", align_bytes=ALIGN)
        d_woven = [keep.tile([P, PACK * HALF], BF16, name=f"d_woven{h}", align_bytes=ALIGN) for h in range(2)]
        early_pair = keep.tile([P, 2 * HALF], F32, name="early_pair", align_bytes=ALIGN)
        late_pair = keep.tile([P, 2 * HALF], F32, name="late_pair", align_bytes=ALIGN)
        diff = {
            (0, 0): early_pair[:],
            (0, 1): late_pair[:],
            (1, 1): picked[:, (2 * PACK - 1) * HALF : (2 * PACK + 1) * HALF],
            (1, 0): late_pair[:],
        }

        def picked_place(t, h):
            at = (2 * t + 1 - h) * HALF
            return picked[:, at : at + HALF]

        def pick(t, h):
            cols = slice(h * LIST_COLS, (h + 1) * LIST_COLS)
            nc.vector.tensor_copy(picked_place(t, h), planes[t][:].indirect(list2[:, cols]))

        def subtract(t, h):
            cols = slice(h * LIST_COLS, (h + 1) * LIST_COLS)
            nc.vector.tensor_tensor(
                diff[h, t // 2][:, (t % 2) * HALF : (t % 2 + 1) * HALF],
                planes[t][:].indirect(list1[:, cols]),
                picked_place(t, h),
                SUB,
            )

        def pair_views(h, u, cols):
            return (
                d_woven[h][:].rearrange("p (c u e) -> p u c e", u=2, e=2)[:, u, cols, :],
                diff[h, u].rearrange("p (e c) -> p c e", e=2)[:, cols, :],
            )

        for t in range(PACK):
            pick(t, 0)
            pick(t, 1)
            subtract(t, 0)
            if t % 2 == 1:
                nc.scalar.copy(*pair_views(0, t // 2, slice(0, HALF)))
        subtract(3, 1)
        subtract(2, 1)
        nc.scalar.copy(*pair_views(1, 1, slice(0, HALF)))

        dealt_words = keep.tile([P, 2 * N], I32, name="dealt_words", align_bytes=ALIGN)
        dealt_scales = keep.tile([P, N], U8, name="dealt_scales", align_bytes=ALIGN)
        for side in (WB_SIDE, W_SIDE):
            nc.gpsimd.tensor_copy(
                dealt_words[:, side * N : (side + 1) * N].rearrange("p (t q) -> p t q", t=PACK),
                raw_words[:, side * N : (side + 1) * N].rearrange("p (q t) -> p t q", t=PACK),
            )
        nc.gpsimd.tensor_copy(
            dealt_scales[:].rearrange("p (t q) -> p t q", t=PACK),
            raw_scales[:].rearrange("p (q t) -> p t q", t=PACK),
        )

        banks = [psum.tile([P, PACK * QUARTER], F32, name=f"bank{b}") for b in range(J // QUARTER)]

        def base_product(b):
            for t in range(PACK):
                at = WB_SIDE * N + t * P
                nc.tensor.matmul_mx(
                    out=banks[b][:, t * QUARTER : (t + 1) * QUARTER],
                    lhsT=dealt_words[:, at : at + P].bitcast(FP8X4),
                    lhsT_scale=dealt_scales[:, t * P : (t + 1) * P],
                    rhs=bx_codes[:, 2 * b * QUARTER : 2 * (b + 1) * QUARTER].bitcast(FP4X4),
                    rhs_scale=bx_plane[:, b * QUARTER : (b + 1) * QUARTER],
                    start=(t == 0),
                    stop=False,
                )

        base_product(0)
        base_product(1)
        d_codes = keep.tile([P, J], U32, name="d_codes", align_bytes=ALIGN)
        d_scales = keep.tile([P, J], U8, name="d_scales", align_bytes=ALIGN)
        y_first = keep.tile([P, PACK, HALF], F32, name="y_first", align_bytes=ALIGN)
        y_last = [keep.tile([P, PACK * QUARTER], F32, name=f"y_last{i}", align_bytes=ALIGN) for i in range(2)]
        y_woven = [keep.tile([P, PACK * HALF], BF16, name=f"y_woven{h}", align_bytes=ALIGN) for h in range(2)]
        y_codes = keep.tile([P, J], U32, name="y_codes", align_bytes=ALIGN)
        y_scales = keep.tile([P, J], U8, name="y_scales", align_bytes=ALIGN)
        out_rows = out_0.rearrange("(p t) j -> p t j", t=PACK)
        out_words = out_1[0].rearrange("p j r -> p (j r)").bitcast(I32)

        def quantize_d(src, cols):
            nc.vector.quantize_mx(out=d_codes[:, cols].bitcast(FP8X4), scales=d_scales[:, cols], in_=src)

        def change_product(b):
            cols = slice(b * QUARTER, (b + 1) * QUARTER)
            for t in range(PACK):
                at = W_SIDE * N + t * P
                nc.tensor.matmul_mx(
                    out=banks[b][:, t * QUARTER : (t + 1) * QUARTER],
                    lhsT=dealt_words[:, at : at + P].bitcast(FP8X4),
                    lhsT_scale=dealt_scales[W_ROW:P, t * P : (t + 1) * P],
                    rhs=d_codes[:, cols].bitcast(FP8X4),
                    rhs_scale=d_scales[:, cols],
                    start=False,
                    stop=(t == PACK - 1),
                )

        def woven_quarters(first, count):
            at = (first % 2) * PACK * QUARTER
            return y_woven[first // 2][:, at : at + count * PACK * QUARTER]

        def weave_y(b, rows):
            nc.vector.tensor_copy(
                woven_quarters(b, 1).rearrange("p (c i t) -> p c t i", t=PACK, i=LINE),
                rows.rearrange("p t (c i) -> p c t i", i=LINE),
            )

        def quantize_y(first, count):
            cols = slice(first * QUARTER, (first + count) * QUARTER)
            nc.vector.quantize_mx(
                out=y_codes[:, cols].bitcast(FP8X4), scales=y_scales[:, cols], in_=woven_quarters(first, count)
            )

        quantize_d(d_woven[0][:], slice(0, HALF))
        subtract(0, 1)
        subtract(1, 1)
        for b in range(2):
            change_product(b)
            nc.scalar.copy(
                y_first[:, :, b * QUARTER : (b + 1) * QUARTER], banks[b][:].rearrange("p (t c) -> p t c", t=PACK)
            )
        nc.sync.dma_start(out_rows[:, :, 0:HALF], y_first[:])
        nc.scalar.copy(
            woven_quarters(0, 1).rearrange("p (c t) -> p c t", t=PACK),
            banks[0][:].rearrange("p (t c) -> p c t", t=PACK),
        )
        base_product(2)
        base_product(3)

        for i in range(2):
            nc.vector.tensor_copy(*pair_views(1, 0, slice(i * QUARTER, (i + 1) * QUARTER)))
        for i in range(2):
            quantize_d(
                d_woven[1][:, i * PACK * QUARTER : (i + 1) * PACK * QUARTER],
                slice(HALF + i * QUARTER, HALF + (i + 1) * QUARTER),
            )
            change_product(2 + i)
        weave_y(1, y_first[:, :, QUARTER:HALF])
        quantize_y(0, 2)
        nc.sync.dma_start(out_words[:, 0:HALF], y_codes[:, 0:HALF].bitcast(I32))
        for i in range(2):
            nc.scalar.copy(y_last[i][:], banks[2 + i][:])
            rows = y_last[i][:].rearrange("p (t c) -> p t c", t=PACK)
            nc.sync.dma_start(out_rows[:, :, HALF + i * QUARTER : HALF + (i + 1) * QUARTER], rows)
            weave_y(2 + i, rows)
        for i in range(2):
            quantize_y(2 + i, 1)
        nc.sync.dma_start(out_words[:, HALF:J], y_codes[:, HALF:J].bitcast(I32))
        for q in range(QUADRANTS):
            queue = nc.sync if q % 2 == 0 else nc.scalar
            queue.dma_start(out_2[0, 4 * q : 4 * q + 4, :].bitcast(I32), y_scales[32 * q : 32 * q + 4, :].bitcast(I32))
